import numpy as np
import ml_dtypes


def mxq(x, axis, fmt="e4m3"):
    dtype, down = {"e4m3": (ml_dtypes.float8_e4m3fn, 7), "e5m2": (ml_dtypes.float8_e5m2, 14)}[fmt]
    v = np.moveaxis(np.asarray(x, np.float32).astype(ml_dtypes.bfloat16).astype(np.float64), axis, -1)
    blocks = v.reshape(v.shape[:-1] + (-1, 32))
    amax = np.abs(blocks).max(-1, keepdims=True)
    byte = np.maximum(np.where(amax > 0, np.frexp(amax)[1] - 1 + 127, 0) - down, 1)
    scale = np.exp2(byte - 127.0)
    codes = (blocks / scale).astype(np.float32).astype(dtype).astype(np.float64)
    return np.moveaxis((codes * scale).reshape(v.shape), -1, axis)


WIDE = False


def mx_kscale(k):
    if not WIDE:
        return np.ones(k)
    levels = np.array([10, -10, 5, -5, 0])
    if k % 512:
        return np.exp2(np.random.permutation(np.resize(levels, k // 32))).repeat(32)
    a = np.empty((k // 512, 16))
    for p in range(k // 512):
        a[p, :8] = np.random.permutation(np.resize(levels, 8))
        for g in range(8):
            far = levels[np.abs(levels - a[p, g]) >= 10]
            a[p, g + 8] = far[np.random.randint(len(far))]
    return np.exp2(a.ravel()).repeat(32)


def f64(x):
    return np.asarray(x).astype(np.float64)


E2M1 = np.array([0.0, 0.5, 1.0, 1.5, 2.0, 3.0, 4.0, 6.0, -0.0, -0.5, -1.0, -1.5, -2.0, -3.0, -4.0, -6.0])


def pack_weight(w, fmt):
    k, n = w.shape
    w = f64(np.asarray(w, np.float32).astype(ml_dtypes.bfloat16)).reshape(k // 32, 32, n)
    amax = np.abs(w).max(1)
    if fmt == "e4m3":
        byte = np.frexp(amax)[1] - 1 + 127 - 7
    else:
        mant, ex = np.frexp(amax / 6.0)
        byte = np.where(mant > 0.5, ex, ex - 1) + 127
    byte = np.clip(np.where(amax > 0, byte, 1), 1, 254)
    scaled = (w * np.exp2(127.0 - byte)[:, None, :]).reshape(k, n).astype(np.float32)
    by_word = np.ascontiguousarray(scaled.reshape(k // 512, 128, 4, n).transpose(0, 1, 3, 2))
    if fmt == "e4m3":
        words = by_word.astype(ml_dtypes.float8_e4m3fn).view(np.uint8)
    else:
        c = by_word.astype(ml_dtypes.float4_e2m1fn).view(np.uint8) & 0xF
        words = (c[..., 0::2] | (c[..., 1::2] << 4)).reshape(k // 512, 128, 2 * n)
    return np.ascontiguousarray(words), np.ascontiguousarray(byte.astype(np.uint8).reshape(k // 512, 16, n))


def unpack_weight(words, scales, fmt):
    g, _, n = scales.shape
    words = np.ascontiguousarray(words).reshape(g, 128, n, -1)
    if fmt == "e4m3":
        vals = words.view(ml_dtypes.float8_e4m3fn).astype(np.float64)
    else:
        nib = np.empty((g, 128, n, 4), np.uint8)
        nib[..., 0::2] = words & 0xF
        nib[..., 1::2] = words >> 4
        vals = E2M1[nib]
    vals = vals * np.repeat(np.exp2(scales.astype(np.float64) - 127.0), 8, axis=1)[..., None]
    return vals.transpose(0, 1, 3, 2).reshape(g * 512, n)


def planes(y):
    n, m = y.shape
    v = y.astype(np.float32).astype(ml_dtypes.bfloat16).astype(np.float64).reshape(n // 32, 32, m)
    top = np.abs(v).max(1)
    byte = np.clip(np.where(top > 0, np.frexp(top)[1] - 1 + 127 - 7, 1), 1, 254)
    codes = (v * np.exp2(127.0 - byte)[:, None, :]).reshape(n, m).astype(np.float32).astype(ml_dtypes.float8_e4m3fn).view(np.uint8)
    words = codes.reshape(n // 512, 128, 4, m).transpose(0, 1, 3, 2)
    return np.ascontiguousarray(words), np.ascontiguousarray(byte.astype(np.uint8).reshape(n // 512, 16, m))


K, M, T = 1024, 512, 1024


def setup_inputs():
    n = np.random.standard_normal
    s = mx_kscale(K)[:, None]
    p_w4 = pack_weight(n((K, M)) / np.sqrt(K) / s ** 2, "e2m1")
    p_w8 = pack_weight(n((K, M)) / np.sqrt(K) / s, "e4m3")
    return {
        "x": (n((K, T)) * s).astype(np.float32),
        "w4_words": p_w4[0],
        "w4_scales": p_w4[1],
        "w8_words": p_w8[0],
        "w8_scales": p_w8[1],
        "g": (n((1024, 512))).astype(np.float32),
    }


def reference(x, w4_words, w4_scales, w8_words, w8_scales, g):
    xa_, xb_ = mxq(f64(x) ** 2, 0, "e4m3"), mxq(f64(x), 0, "e4m3")
    w4_ = unpack_weight(w4_words, w4_scales, "e2m1")
    w8_ = unpack_weight(w8_words, w8_scales, "e4m3")
    y = xa_.T @ w4_ + xb_.T @ w8_
    out_0 = f64(g) * y
    return (out_0,) + planes(out_0)

@@ -1,0 +1,179 @@
+from contextlib import ExitStack
+
+import concourse.mybir as mybir
+
+K, M, T = 1024, 512, 1024
+FLOPS = 2 * 2 * K * M * T
+
+F32 = mybir.dt.float32
+BF16 = mybir.dt.bfloat16
+I32 = mybir.dt.int32
+U32 = mybir.dt.uint32
+U8 = mybir.dt.uint8
+FP8X4 = mybir.dt.float8_e4m3fn_x4
+FP4X4 = mybir.dt.float4_e2m1fn_x4
+ACT = mybir.ActivationFunctionType
+ALU = mybir.AluOpType
+
+P = 128
+PACK = 4
+SPAN = P * PACK
+PASSES = K // SPAN
+GROUPS = T // SPAN
+V_COLS = 320
+
+
+def tile_mix_feat_tm_quadpl_mul_kernel(
+    tc, x, w4_words, w4_scales, w8_words, w8_scales, g, out_0, out_1, out_2
+):
+    nc = tc.nc
+    with ExitStack() as ctx:
+        sb = ctx.enter_context(tc.tile_pool(name="sb", bufs=1))
+        ps = ctx.enter_context(tc.psum_pool(name="ps", bufs=1))
+        ctx.enter_context(tc.manual_schedule())
+
+        chunks = [(a, c) for c in range(PASSES) for a in range(GROUPS)]
+
+        def tiles(name, keys, shape, dtype):
+            return {k: sb.tile(shape, dtype, name="%s_%s" % (name, i), align_bytes=64) for i, k in enumerate(keys)}
+
+        raw = tiles("raw", chunks, [P, PACK, SPAN], F32)
+        lin = tiles("lin", chunks, [P, PACK * SPAN], BF16)
+        sq = tiles("sq", chunks, [P, PACK * SPAN], BF16)
+        lin_codes = tiles("lin_codes", chunks, [P, SPAN], U32)
+        lin_scales = tiles("lin_scales", chunks, [P, SPAN], U8)
+        sq_codes = tiles("sq_codes", chunks, [P, SPAN], U32)
+        sq_scales = tiles("sq_scales", chunks, [P, SPAN], U8)
+        w8 = tiles("w8", range(PASSES), [P, M], U32)
+        w4 = sb.tile([P, PASSES, 2 * M], U8, align_bytes=64)
+        w8_plane = sb.tile([P, PASSES, M], U8, align_bytes=64)
+        w4_plane = sb.tile([P, PASSES, M], U8, align_bytes=64)
+        gate = tiles("gate", range(GROUPS), [P, PACK, M], F32)
+        res = tiles("res", range(GROUPS), [P, PACK, M], F32)
+        res_bf = tiles("res_bf", range(GROUPS), [P, M * PACK], BF16)
+        res_codes = tiles("res_codes", range(GROUPS), [P, M], U32)
+        res_plane = sb.tile([P, GROUPS, M], U8, align_bytes=64)
+        acc = {(a, r): ps.tile([P, M], F32, name="acc_%d_%d" % (a, r)) for a in range(GROUPS) for r in range(PACK)}
+
+        def load_x(a, c):
+            rows = x[c * SPAN:(c + 1) * SPAN, a * SPAN:(a + 1) * SPAN]
+            nc.sync.dma_start(out=raw[a, c][:], in_=rows.rearrange("(p j) t -> p j t", j=PACK))
+
+        def load_w8(c):
+            nc.sync.dma_start(out=w8[c][:].bitcast(I32), in_=w8_words[c].rearrange("p n i -> p (n i)").bitcast(I32))
+
+        def token_rows(dram, a, half):
+            view = dram[a * SPAN:(a + 1) * SPAN, :].rearrange("(p r) n -> p r n", r=PACK)
+            return view[:, 2 * half:2 * half + 2, :]
+
+        def load_plane(queue, plane, scales):
+            by_row = scales.rearrange("c (q r) n -> r q c n", r=4)
+            for r in range(4):
+                queue.dma_start(out=plane[r:P:32, :, :].bitcast(I32), in_=by_row[r].bitcast(I32))
+
+        def dealt(a, c, dst, half):
+            src = raw[a, c][:].rearrange("p j (m r) -> p m j r", r=PACK)[:, :, :, 2 * half:2 * half + 2]
+            out = dst[a, c][:].rearrange("p (r m j) -> p m j r", r=PACK, j=PACK)[:, :, :, 2 * half:2 * half + 2]
+            return out, src
+
+        def cast_lin(a, c, half):
+            out, src = dealt(a, c, lin, half)
+            nc.vector.tensor_copy(out=out, in_=src)
+
+        def cast_sq(a, c, half):
+            out, src = dealt(a, c, sq, half)
+            nc.scalar.activation(out=out, in_=src, func=ACT.Square)
+
+        def quantize(src, codes, scales, a, c, half):
+            cols = slice(half * SPAN // 2, (half + 1) * SPAN // 2)
+            nc.vector.quantize_mx(
+                out=codes[a, c][:, cols].bitcast(FP8X4),
+                scales=scales[a, c][:, cols],
+                in_=src[a, c][:, PACK * cols.start:PACK * cols.stop],
+            )
+
+        def multiply(a, c, r):
+            cols = slice(r * P, (r + 1) * P)
+            nc.tensor.matmul_mx(
+                out=acc[a, r][:],
+                lhsT=lin_codes[a, c][:, cols].bitcast(FP8X4),
+                lhsT_scale=lin_scales[a, c][:, cols],
+                rhs=w8[c][:].bitcast(FP8X4),
+                rhs_scale=w8_plane[:, c, :],
+                start=(c == 0),
+                stop=False,
+            )
+            nc.tensor.matmul_mx(
+                out=acc[a, r][:],
+                lhsT=sq_codes[a, c][:, cols].bitcast(FP8X4),
+                lhsT_scale=sq_scales[a, c][:, cols],
+                rhs=w4[:, c, :].bitcast(FP4X4),
+                rhs_scale=w4_plane[:, c, :],
+                start=False,
+                stop=(c == PASSES - 1),
+            )
+
+        def gate_result(a, r):
+            nc.vector.tensor_tensor(out=res[a][:, r, :], in0=acc[a, r][:], in1=gate[a][:, r, :], op=ALU.mult)
+
+        def store_result(a, half):
+            nc.sync.dma_start(out=token_rows(out_0, a, half), in_=res[a][:, 2 * half:2 * half + 2, :])
+
+        def interleaved(a, lo, hi):
+            src = res[a][:, :, lo:hi].rearrange("p r (u i) -> p u r i", i=4)
+            out = res_bf[a][:, PACK * lo:PACK * hi].rearrange("p (u i r) -> p u r i", i=4, r=PACK)
+            return out, src
+
+        def quantize_result(a):
+            nc.vector.quantize_mx(out=res_codes[a][:].bitcast(FP8X4), scales=res_plane[:, a, :], in_=res_bf[a][:])
+
+        def store_codes(a):
+            nc.sync.dma_start(
+                out=out_1[a].rearrange("p n i -> p (n i)").bitcast(I32), in_=res_codes[a][:].bitcast(I32)
+            )
+
+        nc.vector.memset(w8_plane[:].bitcast(I32), 0)
+        nc.gpsimd.memset(w4_plane[:].bitcast(I32), 0)
+        load_x(0, 0)
+        load_x(1, 0)
+        load_plane(nc.sync, w8_plane, w8_scales)
+        load_w8(0)
+        nc.sync.dma_start(out=w4[:].bitcast(I32), in_=w4_words.rearrange("c p b -> p c b").bitcast(I32))
+        load_plane(nc.gpsimd, w4_plane, w4_scales)
+        load_x(0, 1)
+        load_x(1, 1)
+        load_w8(1)
+        for a in range(GROUPS):
+            for half in range(2):
+                nc.sync.dma_start(out=gate[a][:, 2 * half:2 * half + 2, :], in_=token_rows(g, a, half))
+
+        for a, c in chunks:
+            for half in range(2):
+                cast_sq(a, c, half)
+                cast_lin(a, c, half)
+            for half in range(2):
+                quantize(lin, lin_codes, lin_scales, a, c, half)
+                quantize(sq, sq_codes, sq_scales, a, c, half)
+                multiply(a, c, 2 * half)
+                multiply(a, c, 2 * half + 1)
+
+        for a in range(GROUPS):
+            for half in range(2):
+                gate_result(a, 2 * half)
+                gate_result(a, 2 * half + 1)
+                store_result(a, half)
+            if a == 0:
+                out, src = interleaved(0, 0, M)
+                nc.scalar.copy(out=out, in_=src)
+        out, src = interleaved(1, V_COLS, M)
+        nc.scalar.copy(out=out, in_=src)
+        out, src = interleaved(1, 0, V_COLS)
+        nc.vector.tensor_copy(out=out, in_=src)
+        for a in range(GROUPS):
+            quantize_result(a)
+            store_codes(a)
+        for q in range(4):
+            nc.scalar.dma_start(
+                out=out_2[:, 4 * q:4 * q + 4, :].rearrange("a r n -> r a n").bitcast(I32),
+                in_=res_plane[32 * q:32 * q + 4, :, :].bitcast(I32),
+            )

@@ -21,6 +21,8 @@ SPAN = P * PACK
 PASSES = K // SPAN
 GROUPS = T // SPAN
 V_COLS = 320
+W8_ROW = 4
+RES_ROW = 8
 
 
 def tile_mix_feat_tm_quadpl_mul_kernel(
@@ -46,8 +48,7 @@ def tile_mix_feat_tm_quadpl_mul_kernel(
         sq_scales = tiles("sq_scales", chunks, [P, SPAN], U8)
         w8 = tiles("w8", range(PASSES), [P, M], U32)
         w4 = sb.tile([P, PASSES, 2 * M], U8, align_bytes=64)
-        w8_plane = sb.tile([P, PASSES, M], U8, align_bytes=64)
-        w4_plane = sb.tile([P, PASSES, M], U8, align_bytes=64)
+        w_plane = sb.tile([P, PASSES, M], U8, align_bytes=64)
         gate = tiles("gate", range(GROUPS), [P, PACK, M], F32)
         res = tiles("res", range(GROUPS), [P, PACK, M], F32)
         res_bf = tiles("res_bf", range(GROUPS), [P, M * PACK], BF16)
@@ -66,10 +67,10 @@ def tile_mix_feat_tm_quadpl_mul_kernel(
             view = dram[a * SPAN:(a + 1) * SPAN, :].rearrange("(p r) n -> p r n", r=PACK)
             return view[:, 2 * half:2 * half + 2, :]
 
-        def load_plane(queue, plane, scales):
+        def load_plane(first, scales):
             by_row = scales.rearrange("c (q r) n -> r q c n", r=4)
             for r in range(4):
-                queue.dma_start(out=plane[r:P:32, :, :].bitcast(I32), in_=by_row[r].bitcast(I32))
+                nc.sync.dma_start(out=w_plane[first + r:P:32, :, :].bitcast(I32), in_=by_row[r].bitcast(I32))
 
         def dealt(a, c, dst, half):
             src = raw[a, c][:].rearrange("p j (m r) -> p m j r", r=PACK)[:, :, :, 2 * half:2 * half + 2]
@@ -99,7 +100,7 @@ def tile_mix_feat_tm_quadpl_mul_kernel(
                 lhsT=lin_codes[a, c][:, cols].bitcast(FP8X4),
                 lhsT_scale=lin_scales[a, c][:, cols],
                 rhs=w8[c][:].bitcast(FP8X4),
-                rhs_scale=w8_plane[:, c, :],
+                rhs_scale=w_plane[W8_ROW:P, c, :],
                 start=(c == 0),
                 stop=False,
             )
@@ -108,7 +109,7 @@ def tile_mix_feat_tm_quadpl_mul_kernel(
                 lhsT=sq_codes[a, c][:, cols].bitcast(FP8X4),
                 lhsT_scale=sq_scales[a, c][:, cols],
                 rhs=w4[:, c, :].bitcast(FP4X4),
-                rhs_scale=w4_plane[:, c, :],
+                rhs_scale=w_plane[:, c, :],
                 start=False,
                 stop=(c == PASSES - 1),
             )
@@ -125,41 +126,54 @@ def tile_mix_feat_tm_quadpl_mul_kernel(
             return out, src
 
         def quantize_result(a):
-            nc.vector.quantize_mx(out=res_codes[a][:].bitcast(FP8X4), scales=res_plane[:, a, :], in_=res_bf[a][:])
+            nc.vector.quantize_mx(out=res_codes[a][:].bitcast(FP8X4), scales=res_plane[RES_ROW:P, a, :], in_=res_bf[a][:])
 
         def store_codes(a):
             nc.sync.dma_start(
                 out=out_1[a].rearrange("p n i -> p (n i)").bitcast(I32), in_=res_codes[a][:].bitcast(I32)
             )
 
-        nc.vector.memset(w8_plane[:].bitcast(I32), 0)
-        nc.gpsimd.memset(w4_plane[:].bitcast(I32), 0)
+        def load_gate(a, half):
+            nc.sync.dma_start(out=gate[a][:, 2 * half:2 * half + 2, :], in_=token_rows(g, a, half))
+
+        nc.vector.memset(w_plane[:].bitcast(I32), 0)
         load_x(0, 0)
+        load_plane(W8_ROW, w8_scales)
         load_x(1, 0)
-        load_plane(nc.sync, w8_plane, w8_scales)
         load_w8(0)
         nc.sync.dma_start(out=w4[:].bitcast(I32), in_=w4_words.rearrange("c p b -> p c b").bitcast(I32))
-        load_plane(nc.gpsimd, w4_plane, w4_scales)
+        load_plane(0, w4_scales)
         load_x(0, 1)
         load_x(1, 1)
         load_w8(1)
-        for a in range(GROUPS):
-            for half in range(2):
-                nc.sync.dma_start(out=gate[a][:, 2 * half:2 * half + 2, :], in_=token_rows(g, a, half))
+        load_gate(0, 0)
+        load_gate(0, 1)
+        load_gate(1, 0)
+        load_gate(1, 1)
 
-        for a, c in chunks:
-            for half in range(2):
-                cast_sq(a, c, half)
-                cast_lin(a, c, half)
-            for half in range(2):
-                quantize(lin, lin_codes, lin_scales, a, c, half)
-                quantize(sq, sq_codes, sq_scales, a, c, half)
-                multiply(a, c, 2 * half)
-                multiply(a, c, 2 * half + 1)
+        def finish(a, c):
+            quantize(sq, sq_codes, sq_scales, a, c, 1)
+            multiply(a, c, 2)
+            multiply(a, c, 3)
+
+        for i, (a, c) in enumerate(chunks):
+            cast_sq(a, c, 0)
+            cast_sq(a, c, 1)
+            cast_lin(a, c, 0)
+            if i > 0:
+                finish(*chunks[i - 1])
+            cast_lin(a, c, 1)
+            quantize(lin, lin_codes, lin_scales, a, c, 0)
+            quantize(sq, sq_codes, sq_scales, a, c, 0)
+            multiply(a, c, 0)
+            multiply(a, c, 1)
+            quantize(lin, lin_codes, lin_scales, a, c, 1)
 
         for a in range(GROUPS):
             for half in range(2):
                 gate_result(a, 2 * half)
+                if a == 0 and half == 0:
+                    finish(*chunks[-1])
                 gate_result(a, 2 * half + 1)
                 store_result(a, half)
             if a == 0:
@@ -175,5 +189,5 @@ def tile_mix_feat_tm_quadpl_mul_kernel(
         for q in range(4):
             nc.scalar.dma_start(
                 out=out_2[:, 4 * q:4 * q + 4, :].rearrange("a r n -> r a n").bitcast(I32),
-                in_=res_plane[32 * q:32 * q + 4, :, :].bitcast(I32),
+                in_=res_plane[32 * q + RES_ROW:32 * q + RES_ROW + 4, :, :].bitcast(I32),
             )

@@ -39,7 +39,8 @@ def tile_mix_feat_tm_quadpl_mul_kernel(
         def tiles(name, keys, shape, dtype):
             return {k: sb.tile(shape, dtype, name="%s_%s" % (name, i), align_bytes=64) for i, k in enumerate(keys)}
 
-        raw = tiles("raw", chunks, [P, PACK, SPAN], F32)
+        raw_tiles = tiles("raw", chunks, [P, PACK, SPAN], F32)
+        raw = {k: raw_tiles[k][:] for k in chunks}
         lin = tiles("lin", chunks, [P, PACK * SPAN], BF16)
         sq = tiles("sq", chunks, [P, PACK * SPAN], BF16)
         lin_codes = tiles("lin_codes", chunks, [P, SPAN], U32)
@@ -48,7 +49,7 @@ def tile_mix_feat_tm_quadpl_mul_kernel(
         sq_scales = tiles("sq_scales", chunks, [P, SPAN], U8)
         w8 = tiles("w8", range(PASSES), [P, M], U32)
         w4 = sb.tile([P, PASSES, 2 * M], U8, align_bytes=64)
-        w_plane = sb.tile([P, PASSES, M], U8, align_bytes=64)
+        w_plane = tiles("w_plane", range(2), [P, PASSES, M], U8)
         gate = tiles("gate", range(GROUPS), [P, PACK, M], F32)
         res = tiles("res", range(GROUPS), [P, PACK, M], F32)
         res_bf = tiles("res_bf", range(GROUPS), [P, M * PACK], BF16)
@@ -56,9 +57,9 @@ def tile_mix_feat_tm_quadpl_mul_kernel(
         res_plane = sb.tile([P, GROUPS, M], U8, align_bytes=64)
         acc = {(a, r): ps.tile([P, M], F32, name="acc_%d_%d" % (a, r)) for a in range(GROUPS) for r in range(PACK)}
 
-        def load_x(a, c):
-            rows = x[c * SPAN:(c + 1) * SPAN, a * SPAN:(a + 1) * SPAN]
-            nc.sync.dma_start(out=raw[a, c][:], in_=rows.rearrange("(p j) t -> p j t", j=PACK))
+        def load_x(dst, c, lo, hi):
+            rows = x[c * SPAN:(c + 1) * SPAN, lo:hi]
+            nc.sync.dma_start(out=dst, in_=rows.rearrange("(p j) t -> p j t", j=PACK))
 
         def load_w8(c):
             nc.sync.dma_start(out=w8[c][:].bitcast(I32), in_=w8_words[c].rearrange("p n i -> p (n i)").bitcast(I32))
@@ -67,19 +68,23 @@ def tile_mix_feat_tm_quadpl_mul_kernel(
             view = dram[a * SPAN:(a + 1) * SPAN, :].rearrange("(p r) n -> p r n", r=PACK)
             return view[:, 2 * half:2 * half + 2, :]
 
-        def load_plane(first, scales):
+        def load_plane(w, first, scales):
             by_row = scales.rearrange("c (q r) n -> r q c n", r=4)
             for r in range(4):
-                nc.sync.dma_start(out=w_plane[first + r:P:32, :, :].bitcast(I32), in_=by_row[r].bitcast(I32))
+                nc.sync.dma_start(out=w_plane[w][first + r:P:32, :, :].bitcast(I32), in_=by_row[r].bitcast(I32))
 
         def dealt(a, c, dst, half):
-            src = raw[a, c][:].rearrange("p j (m r) -> p m j r", r=PACK)[:, :, :, 2 * half:2 * half + 2]
+            src = raw[a, c].rearrange("p j (m r) -> p m j r", r=PACK)[:, :, :, 2 * half:2 * half + 2]
             out = dst[a, c][:].rearrange("p (r m j) -> p m j r", r=PACK, j=PACK)[:, :, :, 2 * half:2 * half + 2]
             return out, src
 
         def cast_lin(a, c, half):
             out, src = dealt(a, c, lin, half)
             nc.vector.tensor_copy(out=out, in_=src)
+
+        def cast_lin_scalar(a, c, half):
+            out, src = dealt(a, c, lin, half)
+            nc.scalar.copy(out=out, in_=src)
 
         def cast_sq(a, c, half):
             out, src = dealt(a, c, sq, half)
@@ -93,23 +98,26 @@ def tile_mix_feat_tm_quadpl_mul_kernel(
                 in_=src[a, c][:, PACK * cols.start:PACK * cols.stop],
             )
 
-        def multiply(a, c, r):
+        def pass_lin(a, c, r):
             cols = slice(r * P, (r + 1) * P)
             nc.tensor.matmul_mx(
                 out=acc[a, r][:],
                 lhsT=lin_codes[a, c][:, cols].bitcast(FP8X4),
                 lhsT_scale=lin_scales[a, c][:, cols],
                 rhs=w8[c][:].bitcast(FP8X4),
-                rhs_scale=w_plane[W8_ROW:P, c, :],
+                rhs_scale=w_plane[0][W8_ROW:P, c, :],
                 start=(c == 0),
                 stop=False,
             )
+
+        def pass_sq(a, c, r):
+            cols = slice(r * P, (r + 1) * P)
             nc.tensor.matmul_mx(
                 out=acc[a, r][:],
                 lhsT=sq_codes[a, c][:, cols].bitcast(FP8X4),
                 lhsT_scale=sq_scales[a, c][:, cols],
                 rhs=w4[:, c, :].bitcast(FP4X4),
-                rhs_scale=w_plane[:, c, :],
+                rhs_scale=w_plane[1][:, c, :],
                 start=False,
                 stop=(c == PASSES - 1),
             )
@@ -136,49 +144,74 @@ def tile_mix_feat_tm_quadpl_mul_kernel(
         def load_gate(a, half):
             nc.sync.dma_start(out=gate[a][:, 2 * half:2 * half + 2, :], in_=token_rows(g, a, half))
 
-        nc.vector.memset(w_plane[:].bitcast(I32), 0)
-        load_x(0, 0)
-        load_plane(W8_ROW, w8_scales)
-        load_x(1, 0)
+        nc.vector.memset(w_plane[0][:].bitcast(I32), 0)
+        nc.vector.memset(w_plane[1][:].bitcast(I32), 0)
+        load_x(raw[0, 0], 0, 0, SPAN)
         load_w8(0)
+        load_plane(0, W8_ROW, w8_scales)
+        load_x(raw[1, 0], 0, SPAN, T)
         nc.sync.dma_start(out=w4[:].bitcast(I32), in_=w4_words.rearrange("c p b -> p c b").bitcast(I32))
-        load_plane(0, w4_scales)
-        load_x(0, 1)
-        load_x(1, 1)
+        load_plane(1, 0, w4_scales)
+        load_x(raw[0, 1], 1, 0, SPAN)
+        load_x(raw[1, 1], 1, SPAN, T)
         load_w8(1)
-        load_gate(0, 0)
-        load_gate(0, 1)
-        load_gate(1, 0)
-        load_gate(1, 1)
+        for a in range(GROUPS):
+            for half in range(2):
+                load_gate(a, half)
 
-        def finish(a, c):
-            quantize(sq, sq_codes, sq_scales, a, c, 1)
-            multiply(a, c, 2)
-            multiply(a, c, 3)
+        def q_lin(a, c, half):
+            quantize(lin, lin_codes, lin_scales, a, c, half)
 
-        for i, (a, c) in enumerate(chunks):
+        def q_sq(a, c, half):
+            quantize(sq, sq_codes, sq_scales, a, c, half)
+
+        def both(a, c, r):
+            pass_lin(a, c, r)
+            pass_sq(a, c, r)
+
+        for i, (a, c) in enumerate(chunks[:-1]):
             cast_sq(a, c, 0)
             cast_sq(a, c, 1)
             cast_lin(a, c, 0)
             if i > 0:
-                finish(*chunks[i - 1])
+                b = chunks[i - 1][0]
+                q_sq(b, 0, 1)
+                for r in range(PACK):
+                    pass_sq(b, 0, r)
             cast_lin(a, c, 1)
-            quantize(lin, lin_codes, lin_scales, a, c, 0)
-            quantize(sq, sq_codes, sq_scales, a, c, 0)
-            multiply(a, c, 0)
-            multiply(a, c, 1)
-            quantize(lin, lin_codes, lin_scales, a, c, 1)
+            q_sq(a, c, 0)
+            nc.vector.quantize_mx(out=lin_codes[a, c][:].bitcast(FP8X4), scales=lin_scales[a, c][:], in_=lin[a, c][:])
+            if c == 0:
+                for r in range(PACK):
+                    pass_lin(a, 0, r)
 
-        for a in range(GROUPS):
-            for half in range(2):
-                gate_result(a, 2 * half)
-                if a == 0 and half == 0:
-                    finish(*chunks[-1])
-                gate_result(a, 2 * half + 1)
-                store_result(a, half)
-            if a == 0:
-                out, src = interleaved(0, 0, M)
-                nc.scalar.copy(out=out, in_=src)
+        cast_sq(1, 1, 0)
+        cast_sq(1, 1, 1)
+        cast_lin_scalar(1, 1, 1)
+        cast_lin(1, 1, 0)
+        q_sq(0, 1, 1)
+        for r in range(PACK):
+            both(0, 1, r)
+        q_lin(1, 1, 0)
+        q_sq(1, 1, 0)
+        both(1, 1, 0)
+        both(1, 1, 1)
+        gate_result(0, 0)
+        gate_result(0, 1)
+        store_result(0, 0)
+        q_sq(1, 1, 1)
+        gate_result(0, 2)
+        q_lin(1, 1, 1)
+        both(1, 1, 2)
+        both(1, 1, 3)
+        gate_result(0, 3)
+        store_result(0, 1)
+        out, src = interleaved(0, 0, M)
+        nc.scalar.copy(out=out, in_=src)
+        for half in range(2):
+            gate_result(1, 2 * half)
+            gate_result(1, 2 * half + 1)
+            store_result(1, half)
         out, src = interleaved(1, V_COLS, M)
         nc.scalar.copy(out=out, in_=src)
         out, src = interleaved(1, 0, V_COLS)

@@ -20,7 +20,6 @@ PACK = 4
 SPAN = P * PACK
 PASSES = K // SPAN
 GROUPS = T // SPAN
-V_COLS = 320
 W8_ROW = 4
 RES_ROW = 8
 
@@ -48,7 +47,7 @@ def tile_mix_feat_tm_quadpl_mul_kernel(
         sq_codes = tiles("sq_codes", chunks, [P, SPAN], U32)
         sq_scales = tiles("sq_scales", chunks, [P, SPAN], U8)
         w8 = tiles("w8", range(PASSES), [P, M], U32)
-        w4 = sb.tile([P, PASSES, 2 * M], U8, align_bytes=64)
+        w4 = tiles("w4", range(PASSES), [P, 2 * M], U8)
         w_plane = tiles("w_plane", range(2), [P, PASSES, M], U8)
         gate = tiles("gate", range(GROUPS), [P, PACK, M], F32)
         res = tiles("res", range(GROUPS), [P, PACK, M], F32)
@@ -64,9 +63,12 @@ def tile_mix_feat_tm_quadpl_mul_kernel(
         def load_w8(c):
             nc.sync.dma_start(out=w8[c][:].bitcast(I32), in_=w8_words[c].rearrange("p n i -> p (n i)").bitcast(I32))
 
-        def token_rows(dram, a, half):
+        def load_w4(c):
+            nc.sync.dma_start(out=w4[c][:].bitcast(I32), in_=w4_words[c].bitcast(I32))
+
+        def token_rows(dram, a, lo, hi):
             view = dram[a * SPAN:(a + 1) * SPAN, :].rearrange("(p r) n -> p r n", r=PACK)
-            return view[:, 2 * half:2 * half + 2, :]
+            return view[:, lo:hi, :]
 
         def load_plane(w, first, scales):
             by_row = scales.rearrange("c (q r) n -> r q c n", r=4)
@@ -116,33 +118,46 @@ def tile_mix_feat_tm_quadpl_mul_kernel(
                 out=acc[a, r][:],
                 lhsT=sq_codes[a, c][:, cols].bitcast(FP8X4),
                 lhsT_scale=sq_scales[a, c][:, cols],
-                rhs=w4[:, c, :].bitcast(FP4X4),
+                rhs=w4[c][:].bitcast(FP4X4),
                 rhs_scale=w_plane[1][:, c, :],
                 start=False,
                 stop=(c == PASSES - 1),
             )
 
-        def gate_result(a, r):
-            nc.vector.tensor_tensor(out=res[a][:, r, :], in0=acc[a, r][:], in1=gate[a][:, r, :], op=ALU.mult)
+        def gate_result(a, r, lo=0, hi=M):
+            nc.vector.tensor_tensor(
+                out=res[a][:, r, lo:hi], in0=acc[a, r][:, lo:hi], in1=gate[a][:, r, lo:hi], op=ALU.mult
+            )
 
         def store_result(a, half):
-            nc.sync.dma_start(out=token_rows(out_0, a, half), in_=res[a][:, 2 * half:2 * half + 2, :])
+            nc.sync.dma_start(out=token_rows(out_0, a, 2 * half, 2 * half + 2), in_=res[a][:, 2 * half:2 * half + 2, :])
 
         def interleaved(a, lo, hi):
             src = res[a][:, :, lo:hi].rearrange("p r (u i) -> p u r i", i=4)
             out = res_bf[a][:, PACK * lo:PACK * hi].rearrange("p (u i r) -> p u r i", i=4, r=PACK)
             return out, src
 
-        def quantize_result(a):
-            nc.vector.quantize_mx(out=res_codes[a][:].bitcast(FP8X4), scales=res_plane[RES_ROW:P, a, :], in_=res_bf[a][:])
+        def round_scalar(a, lo, hi):
+            out, src = interleaved(a, lo, hi)
+            nc.scalar.copy(out=out, in_=src)
 
-        def store_codes(a):
-            nc.sync.dma_start(
-                out=out_1[a].rearrange("p n i -> p (n i)").bitcast(I32), in_=res_codes[a][:].bitcast(I32)
+        def round_vector(a, lo, hi):
+            out, src = interleaved(a, lo, hi)
+            nc.vector.tensor_copy(out=out, in_=src)
+
+        def quantize_result(a, lo, hi):
+            nc.vector.quantize_mx(
+                out=res_codes[a][:, lo:hi].bitcast(FP8X4),
+                scales=res_plane[RES_ROW:P, a, lo:hi],
+                in_=res_bf[a][:, PACK * lo:PACK * hi],
             )
 
-        def load_gate(a, half):
-            nc.sync.dma_start(out=gate[a][:, 2 * half:2 * half + 2, :], in_=token_rows(g, a, half))
+        def store_codes(a, lo, hi):
+            words = out_1[a].rearrange("p n i -> p (n i)").bitcast(I32)
+            nc.sync.dma_start(out=words[:, lo:hi], in_=res_codes[a][:, lo:hi].bitcast(I32))
+
+        def load_gate(a, lo, hi):
+            nc.sync.dma_start(out=gate[a][:, lo:hi, :], in_=token_rows(g, a, lo, hi))
 
         nc.vector.memset(w_plane[0][:].bitcast(I32), 0)
         nc.vector.memset(w_plane[1][:].bitcast(I32), 0)
@@ -150,14 +165,17 @@ def tile_mix_feat_tm_quadpl_mul_kernel(
         load_w8(0)
         load_plane(0, W8_ROW, w8_scales)
         load_x(raw[1, 0], 0, SPAN, T)
-        nc.sync.dma_start(out=w4[:].bitcast(I32), in_=w4_words.rearrange("c p b -> p c b").bitcast(I32))
-        load_plane(1, 0, w4_scales)
         load_x(raw[0, 1], 1, 0, SPAN)
+        load_w4(0)
+        load_plane(1, 0, w4_scales)
         load_x(raw[1, 1], 1, SPAN, T)
         load_w8(1)
-        for a in range(GROUPS):
-            for half in range(2):
-                load_gate(a, half)
+        load_w4(1)
+        load_gate(0, 0, 1)
+        load_gate(0, 1, 2)
+        load_gate(0, 2, 4)
+        load_gate(1, 0, 2)
+        load_gate(1, 2, 4)
 
         def q_lin(a, c, half):
             quantize(lin, lin_codes, lin_scales, a, c, half)
@@ -174,16 +192,16 @@ def tile_mix_feat_tm_quadpl_mul_kernel(
             cast_sq(a, c, 1)
             cast_lin(a, c, 0)
             if i > 0:
-                b = chunks[i - 1][0]
-                q_sq(b, 0, 1)
-                for r in range(PACK):
-                    pass_sq(b, 0, r)
+                q_sq(chunks[i - 1][0], 0, 1)
             cast_lin(a, c, 1)
             q_sq(a, c, 0)
             nc.vector.quantize_mx(out=lin_codes[a, c][:].bitcast(FP8X4), scales=lin_scales[a, c][:], in_=lin[a, c][:])
             if c == 0:
                 for r in range(PACK):
                     pass_lin(a, 0, r)
+        for a in range(GROUPS):
+            for r in range(PACK):
+                pass_sq(a, 0, r)
 
         cast_sq(1, 1, 0)
         cast_sq(1, 1, 1)
@@ -199,26 +217,36 @@ def tile_mix_feat_tm_quadpl_mul_kernel(
         gate_result(0, 0)
         gate_result(0, 1)
         store_result(0, 0)
+        H = M // 2
+        Q3 = 3 * M // 4
         q_sq(1, 1, 1)
-        gate_result(0, 2)
+        gate_result(0, 2, 0, H)
+        gate_result(0, 3, 0, H)
+        round_scalar(0, 0, H)
         q_lin(1, 1, 1)
         both(1, 1, 2)
         both(1, 1, 3)
-        gate_result(0, 3)
+        gate_result(0, 2, H, M)
+        gate_result(0, 3, H, M)
         store_result(0, 1)
-        out, src = interleaved(0, 0, M)
-        nc.scalar.copy(out=out, in_=src)
-        for half in range(2):
-            gate_result(1, 2 * half)
-            gate_result(1, 2 * half + 1)
-            store_result(1, half)
-        out, src = interleaved(1, V_COLS, M)
-        nc.scalar.copy(out=out, in_=src)
-        out, src = interleaved(1, 0, V_COLS)
-        nc.vector.tensor_copy(out=out, in_=src)
-        for a in range(GROUPS):
-            quantize_result(a)
-            store_codes(a)
+        round_scalar(0, H, M)
+        gate_result(1, 0)
+        gate_result(1, 1)
+        store_result(1, 0)
+        gate_result(1, 2, 0, H)
+        gate_result(1, 3, 0, H)
+        round_scalar(1, 0, H)
+        gate_result(1, 2, H, M)
+        gate_result(1, 3, H, M)
+        store_result(1, 1)
+        round_scalar(1, Q3, M)
+        quantize_result(0, 0, M)
+        store_codes(0, 0, M)
+        round_vector(1, H, Q3)
+        quantize_result(1, 0, H)
+        store_codes(1, 0, H)
+        quantize_result(1, H, M)
+        store_codes(1, H, M)
         for q in range(4):
             nc.scalar.dma_start(
                 out=out_2[:, 4 * q:4 * q + 4, :].rearrange("a r n -> r a n").bitcast(I32),

@@ -48,12 +48,13 @@ def tile_mix_feat_tm_quadpl_mul_kernel(
         sq_scales = tiles("sq_scales", chunks, [P, SPAN], U8)
         w8 = tiles("w8", range(PASSES), [P, M], U32)
         w4 = tiles("w4", range(PASSES), [P, 2 * M], U8)
-        w_plane = tiles("w_plane", range(2), [P, PASSES, M], U8)
+        w4_plane = sb.tile([P, PASSES, M], U8, align_bytes=64)
+        w8_plane = sb.tile([P, M], U8, align_bytes=64)
         gate = tiles("gate", range(GROUPS), [P, PACK, M], F32)
         res = tiles("res", range(GROUPS), [P, PACK, M], F32)
         res_bf = tiles("res_bf", range(GROUPS), [P, M * PACK], BF16)
         res_codes = tiles("res_codes", range(GROUPS), [P, M], U32)
-        res_plane = sb.tile([P, GROUPS, M], U8, align_bytes=64)
+        res_plane = sb.tile([P, M], U8, align_bytes=64)
         acc = {(a, r): ps.tile([P, M], F32, name="acc_%d_%d" % (a, r)) for a in range(GROUPS) for r in range(PACK)}
 
         def load_x(dst, c, lo, hi):
@@ -70,10 +71,17 @@ def tile_mix_feat_tm_quadpl_mul_kernel(
             view = dram[a * SPAN:(a + 1) * SPAN, :].rearrange("(p r) n -> p r n", r=PACK)
             return view[:, lo:hi, :]
 
-        def load_plane(w, first, scales):
-            by_row = scales.rearrange("c (q r) n -> r q c n", r=4)
+        def load_w4_plane():
+            by_row = w4_scales.rearrange("c (q r) n -> r q c n", r=4)
             for r in range(4):
-                nc.sync.dma_start(out=w_plane[w][first + r:P:32, :, :].bitcast(I32), in_=by_row[r].bitcast(I32))
+                nc.sync.dma_start(out=w4_plane[r:P:32, :, :].bitcast(I32), in_=by_row[r].bitcast(I32))
+
+        def load_w8_plane():
+            for q in (0, 2, 1, 3):
+                nc.sync.dma_start(
+                    out=w8_plane[32 * q + W8_ROW:32 * q + W8_ROW + 8, :].bitcast(I32),
+                    in_=w8_scales[:, 4 * q:4 * q + 4, :].bitcast(I32),
+                )
 
         def dealt(a, c, dst, half):
             src = raw[a, c].rearrange("p j (m r) -> p m j r", r=PACK)[:, :, :, 2 * half:2 * half + 2]
@@ -107,8 +115,8 @@ def tile_mix_feat_tm_quadpl_mul_kernel(
                 lhsT=lin_codes[a, c][:, cols].bitcast(FP8X4),
                 lhsT_scale=lin_scales[a, c][:, cols],
                 rhs=w8[c][:].bitcast(FP8X4),
-                rhs_scale=w_plane[0][W8_ROW:P, c, :],
-                start=(c == 0),
+                rhs_scale=w8_plane[W8_ROW + 4 * c:P, :],
+                start=False,
                 stop=False,
             )
 
@@ -119,8 +127,8 @@ def tile_mix_feat_tm_quadpl_mul_kernel(
                 lhsT=sq_codes[a, c][:, cols].bitcast(FP8X4),
                 lhsT_scale=sq_scales[a, c][:, cols],
                 rhs=w4[c][:].bitcast(FP4X4),
-                rhs_scale=w_plane[1][:, c, :],
-                start=False,
+                rhs_scale=w4_plane[:, c, :],
+                start=(c == 0),
                 stop=(c == PASSES - 1),
             )
 
@@ -148,7 +156,7 @@ def tile_mix_feat_tm_quadpl_mul_kernel(
         def quantize_result(a, lo, hi):
             nc.vector.quantize_mx(
                 out=res_codes[a][:, lo:hi].bitcast(FP8X4),
-                scales=res_plane[RES_ROW:P, a, lo:hi],
+                scales=res_plane[RES_ROW + 4 * a:P, lo:hi],
                 in_=res_bf[a][:, PACK * lo:PACK * hi],
             )
 
@@ -159,15 +167,15 @@ def tile_mix_feat_tm_quadpl_mul_kernel(
         def load_gate(a, lo, hi):
             nc.sync.dma_start(out=gate[a][:, lo:hi, :], in_=token_rows(g, a, lo, hi))
 
-        nc.vector.memset(w_plane[0][:].bitcast(I32), 0)
-        nc.vector.memset(w_plane[1][:].bitcast(I32), 0)
+        nc.vector.memset(w4_plane[:].bitcast(I32), 0)
+        nc.vector.memset(w8_plane[:].bitcast(I32), 0)
         load_x(raw[0, 0], 0, 0, SPAN)
-        load_w8(0)
-        load_plane(0, W8_ROW, w8_scales)
+        load_w4(0)
+        load_w4_plane()
         load_x(raw[1, 0], 0, SPAN, T)
         load_x(raw[0, 1], 1, 0, SPAN)
-        load_w4(0)
-        load_plane(1, 0, w4_scales)
+        load_w8(0)
+        load_w8_plane()
         load_x(raw[1, 1], 1, SPAN, T)
         load_w8(1)
         load_w4(1)
@@ -187,27 +195,25 @@ def tile_mix_feat_tm_quadpl_mul_kernel(
             pass_lin(a, c, r)
             pass_sq(a, c, r)
 
-        for i, (a, c) in enumerate(chunks[:-1]):
+        for a, c in chunks[:-1]:
             cast_sq(a, c, 0)
             cast_sq(a, c, 1)
             cast_lin(a, c, 0)
-            if i > 0:
-                q_sq(chunks[i - 1][0], 0, 1)
             cast_lin(a, c, 1)
             q_sq(a, c, 0)
             nc.vector.quantize_mx(out=lin_codes[a, c][:].bitcast(FP8X4), scales=lin_scales[a, c][:], in_=lin[a, c][:])
+            q_sq(a, c, 1)
             if c == 0:
                 for r in range(PACK):
-                    pass_lin(a, 0, r)
+                    pass_sq(a, 0, r)
         for a in range(GROUPS):
             for r in range(PACK):
-                pass_sq(a, 0, r)
+                pass_lin(a, 0, r)
 
         cast_sq(1, 1, 0)
         cast_sq(1, 1, 1)
         cast_lin_scalar(1, 1, 1)
         cast_lin(1, 1, 0)
-        q_sq(0, 1, 1)
         for r in range(PACK):
             both(0, 1, r)
         q_lin(1, 1, 0)
@@ -249,6 +255,6 @@ def tile_mix_feat_tm_quadpl_mul_kernel(
         store_codes(1, H, M)
         for q in range(4):
             nc.scalar.dma_start(
-                out=out_2[:, 4 * q:4 * q + 4, :].rearrange("a r n -> r a n").bitcast(I32),
-                in_=res_plane[32 * q + RES_ROW:32 * q + RES_ROW + 4, :, :].bitcast(I32),
+                out=out_2[:, 4 * q:4 * q + 4, :].bitcast(I32),
+                in_=res_plane[32 * q + RES_ROW:32 * q + RES_ROW + 8, :].bitcast(I32),
             )

@@ -137,8 +137,9 @@ def tile_mix_feat_tm_quadpl_mul_kernel(
                 out=res[a][:, r, lo:hi], in0=acc[a, r][:, lo:hi], in1=gate[a][:, r, lo:hi], op=ALU.mult
             )
 
-        def store_result(a, half):
-            nc.sync.dma_start(out=token_rows(out_0, a, 2 * half, 2 * half + 2), in_=res[a][:, 2 * half:2 * half + 2, :])
+        def store_result(a, lo, hi):
+            rows = out_0[a * SPAN:(a + 1) * SPAN, :].rearrange("(p r) n -> p (r n)", r=PACK)
+            nc.sync.dma_start(out=rows[:, lo:hi], in_=res[a][:].rearrange("p r n -> p (r n)")[:, lo:hi])
 
         def interleaved(a, lo, hi):
             src = res[a][:, :, lo:hi].rearrange("p r (u i) -> p u r i", i=4)
@@ -220,13 +221,13 @@ def tile_mix_feat_tm_quadpl_mul_kernel(
         q_sq(1, 1, 0)
         both(1, 1, 0)
         both(1, 1, 1)
+        H = M // 2
+        Q3 = 3 * M // 4 + 32
         gate_result(0, 0)
         gate_result(0, 1)
-        store_result(0, 0)
-        H = M // 2
-        Q3 = 3 * M // 4
         q_sq(1, 1, 1)
         gate_result(0, 2, 0, H)
+        store_result(0, 0, 2 * M + H)
         gate_result(0, 3, 0, H)
         round_scalar(0, 0, H)
         q_lin(1, 1, 1)
@@ -234,25 +235,25 @@ def tile_mix_feat_tm_quadpl_mul_kernel(
         both(1, 1, 3)
         gate_result(0, 2, H, M)
         gate_result(0, 3, H, M)
-        store_result(0, 1)
+        store_result(0, 2 * M + H, 4 * M)
         round_scalar(0, H, M)
         gate_result(1, 0)
+        store_result(1, 0, M)
         gate_result(1, 1)
-        store_result(1, 0)
         gate_result(1, 2, 0, H)
+        store_result(1, M, 2 * M + H)
         gate_result(1, 3, 0, H)
         round_scalar(1, 0, H)
         gate_result(1, 2, H, M)
         gate_result(1, 3, H, M)
-        store_result(1, 1)
+        store_result(1, 2 * M + H, 4 * M)
         round_scalar(1, Q3, M)
         quantize_result(0, 0, M)
         store_codes(0, 0, M)
         round_vector(1, H, Q3)
         quantize_result(1, 0, H)
-        store_codes(1, 0, H)
         quantize_result(1, H, M)
-        store_codes(1, H, M)
+        store_codes(1, 0, M)
         for q in range(4):
             nc.scalar.dma_start(
                 out=out_2[:, 4 * q:4 * q + 4, :].bitcast(I32),

@@ -88,12 +88,18 @@ def tile_mix_feat_tm_quadpl_mul_kernel(
             out = dst[a, c][:].rearrange("p (r m j) -> p m j r", r=PACK, j=PACK)[:, :, :, 2 * half:2 * half + 2]
             return out, src
 
+        def dealt_pairs(a, c, half):
+            pair = slice(2 * half, 2 * half + 2)
+            src = raw[a, c].rearrange("p (h l) (m r) -> p m h r l", l=2, r=PACK)[:, :, :, pair, :]
+            out = lin[a, c][:].rearrange("p (r m h l) -> p m h r l", r=PACK, h=2, l=2)[:, :, :, pair, :]
+            return out, src
+
         def cast_lin(a, c, half):
-            out, src = dealt(a, c, lin, half)
+            out, src = dealt_pairs(a, c, half)
             nc.vector.tensor_copy(out=out, in_=src)
 
         def cast_lin_scalar(a, c, half):
-            out, src = dealt(a, c, lin, half)
+            out, src = dealt_pairs(a, c, half)
             nc.scalar.copy(out=out, in_=src)
 
         def cast_sq(a, c, half):
@@ -142,8 +148,8 @@ def tile_mix_feat_tm_quadpl_mul_kernel(
             nc.sync.dma_start(out=rows[:, lo:hi], in_=res[a][:].rearrange("p r n -> p (r n)")[:, lo:hi])
 
         def interleaved(a, lo, hi):
-            src = res[a][:, :, lo:hi].rearrange("p r (u i) -> p u r i", i=4)
-            out = res_bf[a][:, PACK * lo:PACK * hi].rearrange("p (u i r) -> p u r i", i=4, r=PACK)
+            src = res[a][:, :, lo:hi].rearrange("p (h l) (u i) -> p u h i l", l=2, i=4)
+            out = res_bf[a][:, PACK * lo:PACK * hi].rearrange("p (u i h l) -> p u h i l", i=4, h=2, l=2)
             return out, src
 
         def round_scalar(a, lo, hi):

@@ -22,6 +22,7 @@ PASSES = K // SPAN
 GROUPS = T // SPAN
 W8_ROW = 4
 RES_ROW = 8
+SHIFT = 128
 
 
 def tile_mix_feat_tm_quadpl_mul_kernel(
@@ -48,8 +49,10 @@ def tile_mix_feat_tm_quadpl_mul_kernel(
         sq_scales = tiles("sq_scales", chunks, [P, SPAN], U8)
         w8 = tiles("w8", range(PASSES), [P, M], U32)
         w4 = tiles("w4", range(PASSES), [P, 2 * M], U8)
-        w4_plane = sb.tile([P, PASSES, M], U8, align_bytes=64)
-        w8_plane = sb.tile([P, M], U8, align_bytes=64)
+        w4_plane_tile = sb.tile([P, PASSES * M + 2 * SHIFT], U8, align_bytes=64)
+        w8_plane_tile = sb.tile([P, M + 2 * SHIFT], U8, align_bytes=64)
+        w4_plane = w4_plane_tile[:, SHIFT:SHIFT + PASSES * M].rearrange("p (c n) -> p c n", c=PASSES)
+        w8_plane = w8_plane_tile[:, SHIFT:SHIFT + M]
         gate = tiles("gate", range(GROUPS), [P, PACK, M], F32)
         res = tiles("res", range(GROUPS), [P, PACK, M], F32)
         res_bf = tiles("res_bf", range(GROUPS), [P, M * PACK], BF16)
@@ -174,8 +177,8 @@ def tile_mix_feat_tm_quadpl_mul_kernel(
         def load_gate(a, lo, hi):
             nc.sync.dma_start(out=gate[a][:, lo:hi, :], in_=token_rows(g, a, lo, hi))
 
-        nc.vector.memset(w4_plane[:].bitcast(I32), 0)
-        nc.vector.memset(w8_plane[:].bitcast(I32), 0)
+        nc.vector.memset(w4_plane.bitcast(I32), 0)
+        nc.vector.memset(w8_plane.bitcast(I32), 0)
         load_x(raw[0, 0], 0, 0, SPAN)
         load_w4(0)
         load_w4_plane()

@@ -35,12 +35,15 @@ def tile_mix_feat_tm_quadpl_mul_kernel(
         ctx.enter_context(tc.manual_schedule())
 
         chunks = [(a, c) for c in range(PASSES) for a in range(GROUPS)]
+        pieces = [(0, 0, 0, P), (1, 0, 0, P), (0, 1, 0, P), (1, 1, 0, P)]
 
         def tiles(name, keys, shape, dtype):
             return {k: sb.tile(shape, dtype, name="%s_%s" % (name, i), align_bytes=64) for i, k in enumerate(keys)}
 
-        raw_tiles = tiles("raw", chunks, [P, PACK, SPAN], F32)
-        raw = {k: raw_tiles[k][:] for k in chunks}
+        raw = {
+            k: sb.tile([P, PACK, PACK * (k[3] - k[2])], F32, name="raw_%d" % i, align_bytes=64)
+            for i, k in enumerate(pieces)
+        }
         lin = tiles("lin", chunks, [P, PACK * SPAN], BF16)
         sq = tiles("sq", chunks, [P, PACK * SPAN], BF16)
         lin_codes = tiles("lin_codes", chunks, [P, SPAN], U32)
@@ -48,7 +51,7 @@ def tile_mix_feat_tm_quadpl_mul_kernel(
         sq_codes = tiles("sq_codes", chunks, [P, SPAN], U32)
         sq_scales = tiles("sq_scales", chunks, [P, SPAN], U8)
         w8 = tiles("w8", range(PASSES), [P, M], U32)
-        w4 = tiles("w4", range(PASSES), [P, 2 * M], U8)
+        w4 = sb.tile([P, PASSES * 2 * M], U8, align_bytes=64)
         w4_plane_tile = sb.tile([P, PASSES * M + 2 * SHIFT], U8, align_bytes=64)
         w8_plane_tile = sb.tile([P, M + 2 * SHIFT], U8, align_bytes=64)
         w4_plane = w4_plane_tile[:, SHIFT:SHIFT + PASSES * M].rearrange("p (c n) -> p c n", c=PASSES)
@@ -60,15 +63,17 @@ def tile_mix_feat_tm_quadpl_mul_kernel(
         res_plane = sb.tile([P, M], U8, align_bytes=64)
         acc = {(a, r): ps.tile([P, M], F32, name="acc_%d_%d" % (a, r)) for a in range(GROUPS) for r in range(PACK)}
 
-        def load_x(dst, c, lo, hi):
-            rows = x[c * SPAN:(c + 1) * SPAN, lo:hi]
-            nc.sync.dma_start(out=dst, in_=rows.rearrange("(p j) t -> p j t", j=PACK))
+        def load_x(piece):
+            a, c, lo, hi = piece
+            rows = x[c * SPAN:(c + 1) * SPAN, a * SPAN + PACK * lo:a * SPAN + PACK * hi]
+            nc.sync.dma_start(out=raw[piece][:], in_=rows.rearrange("(p j) t -> p j t", j=PACK))
 
         def load_w8(c):
             nc.sync.dma_start(out=w8[c][:].bitcast(I32), in_=w8_words[c].rearrange("p n i -> p (n i)").bitcast(I32))
 
-        def load_w4(c):
-            nc.sync.dma_start(out=w4[c][:].bitcast(I32), in_=w4_words[c].bitcast(I32))
+        def load_w4(lo, hi):
+            out = w4[:].bitcast(I32).rearrange("p (c n) -> p c n", c=PASSES)
+            nc.sync.dma_start(out=out[:, lo:hi, :], in_=w4_words.bitcast(I32).rearrange("c p n -> p c n")[:, lo:hi, :])
 
         def token_rows(dram, a, lo, hi):
             view = dram[a * SPAN:(a + 1) * SPAN, :].rearrange("(p r) n -> p r n", r=PACK)
@@ -86,38 +91,49 @@ def tile_mix_feat_tm_quadpl_mul_kernel(
                     in_=w8_scales[:, 4 * q:4 * q + 4, :].bitcast(I32),
                 )
 
-        def dealt(a, c, dst, half):
-            src = raw[a, c].rearrange("p j (m r) -> p m j r", r=PACK)[:, :, :, 2 * half:2 * half + 2]
-            out = dst[a, c][:].rearrange("p (r m j) -> p m j r", r=PACK, j=PACK)[:, :, :, 2 * half:2 * half + 2]
-            return out, src
-
-        def dealt_pairs(a, c, half):
+        def dealt(piece, half, lo=None, hi=None):
+            a, c, first, last = piece
+            lo, hi = (first, last) if lo is None else (lo, hi)
             pair = slice(2 * half, 2 * half + 2)
-            src = raw[a, c].rearrange("p (h l) (m r) -> p m h r l", l=2, r=PACK)[:, :, :, pair, :]
-            out = lin[a, c][:].rearrange("p (r m h l) -> p m h r l", r=PACK, h=2, l=2)[:, :, :, pair, :]
+            src = raw[piece][:].rearrange("p j (m r) -> p m j r", r=PACK)[:, lo - first:hi - first, :, pair]
+            out = sq[a, c][:].rearrange("p (r m j) -> p m j r", r=PACK, j=PACK)[:, lo:hi, :, pair]
             return out, src
 
-        def cast_lin(a, c, half):
-            out, src = dealt_pairs(a, c, half)
+        def dealt_pairs(piece, half, lo=None, hi=None):
+            a, c, first, last = piece
+            lo, hi = (first, last) if lo is None else (lo, hi)
+            pair = slice(2 * half, 2 * half + 2)
+            src = raw[piece][:].rearrange("p (h l) (m r) -> p m h r l", l=2, r=PACK)[:, lo - first:hi - first, :, pair, :]
+            out = lin[a, c][:].rearrange("p (r m h l) -> p m h r l", r=PACK, h=2, l=2)[:, lo:hi, :, pair, :]
+            return out, src
+
+        def cast_lin(piece, half, lo=None, hi=None):
+            out, src = dealt_pairs(piece, half, lo, hi)
             nc.vector.tensor_copy(out=out, in_=src)
 
-        def cast_lin_scalar(a, c, half):
-            out, src = dealt_pairs(a, c, half)
+        def cast_lin_scalar(piece, half, lo=None, hi=None):
+            out, src = dealt_pairs(piece, half, lo, hi)
             nc.scalar.copy(out=out, in_=src)
 
-        def cast_sq(a, c, half):
-            out, src = dealt(a, c, sq, half)
+        def cast_sq(piece, half, lo=None, hi=None):
+            out, src = dealt(piece, half, lo, hi)
             nc.scalar.activation(out=out, in_=src, func=ACT.Square)
 
-        def quantize(src, codes, scales, a, c, half):
-            cols = slice(half * SPAN // 2, (half + 1) * SPAN // 2)
+        def quantize(src, codes, scales, a, c, lo, hi):
+            cols = slice(lo * P, hi * P)
             nc.vector.quantize_mx(
                 out=codes[a, c][:, cols].bitcast(FP8X4),
                 scales=scales[a, c][:, cols],
                 in_=src[a, c][:, PACK * cols.start:PACK * cols.stop],
             )
 
-        def pass_lin(a, c, r):
+        def q_lin(a, c, lo, hi):
+            quantize(lin, lin_codes, lin_scales, a, c, lo, hi)
+
+        def q_sq(a, c, lo, hi):
+            quantize(sq, sq_codes, sq_scales, a, c, lo, hi)
+
+        def pass_lin(a, c, r, stop=False):
             cols = slice(r * P, (r + 1) * P)
             nc.tensor.matmul_mx(
                 out=acc[a, r][:],
@@ -126,19 +142,19 @@ def tile_mix_feat_tm_quadpl_mul_kernel(
                 rhs=w8[c][:].bitcast(FP8X4),
                 rhs_scale=w8_plane[W8_ROW + 4 * c:P, :],
                 start=False,
-                stop=False,
+                stop=stop,
             )
 
-        def pass_sq(a, c, r):
+        def pass_sq(a, c, r, stop=False):
             cols = slice(r * P, (r + 1) * P)
             nc.tensor.matmul_mx(
                 out=acc[a, r][:],
                 lhsT=sq_codes[a, c][:, cols].bitcast(FP8X4),
                 lhsT_scale=sq_scales[a, c][:, cols],
-                rhs=w4[c][:].bitcast(FP4X4),
+                rhs=w4[:, 2 * M * c:2 * M * (c + 1)].bitcast(FP4X4),
                 rhs_scale=w4_plane[:, c, :],
                 start=(c == 0),
-                stop=(c == PASSES - 1),
+                stop=stop,
             )
 
         def gate_result(a, r, lo=0, hi=M):
@@ -177,42 +193,50 @@ def tile_mix_feat_tm_quadpl_mul_kernel(
         def load_gate(a, lo, hi):
             nc.sync.dma_start(out=gate[a][:, lo:hi, :], in_=token_rows(g, a, lo, hi))
 
+        def store_scales():
+            for q in range(4):
+                nc.scalar.dma_start(
+                    out=out_2[:, 4 * q:4 * q + 4, :].bitcast(I32),
+                    in_=res_plane[32 * q + RES_ROW:32 * q + RES_ROW + 8, :].bitcast(I32),
+                )
+
+        H = M // 2
+        Q3 = 3 * M // 4 + 32
+        x00, x10, x01, x11 = pieces
+
         nc.vector.memset(w4_plane.bitcast(I32), 0)
         nc.vector.memset(w8_plane.bitcast(I32), 0)
-        load_x(raw[0, 0], 0, 0, SPAN)
-        load_w4(0)
+        load_x(x00)
+        load_w4(0, 1)
         load_w4_plane()
-        load_x(raw[1, 0], 0, SPAN, T)
-        load_x(raw[0, 1], 1, 0, SPAN)
+        load_x(x10)
+        load_x(x01)
         load_w8(0)
         load_w8_plane()
-        load_x(raw[1, 1], 1, SPAN, T)
+        load_x(x11)
         load_w8(1)
-        load_w4(1)
+        load_w4(1, 2)
         load_gate(0, 0, 1)
         load_gate(0, 1, 2)
         load_gate(0, 2, 4)
         load_gate(1, 0, 2)
         load_gate(1, 2, 4)
 
-        def q_lin(a, c, half):
-            quantize(lin, lin_codes, lin_scales, a, c, half)
-
-        def q_sq(a, c, half):
-            quantize(sq, sq_codes, sq_scales, a, c, half)
-
-        def both(a, c, r):
-            pass_lin(a, c, r)
-            pass_sq(a, c, r)
-
-        for a, c in chunks[:-1]:
-            cast_sq(a, c, 0)
-            cast_sq(a, c, 1)
-            cast_lin(a, c, 0)
-            cast_lin(a, c, 1)
-            q_sq(a, c, 0)
-            nc.vector.quantize_mx(out=lin_codes[a, c][:].bitcast(FP8X4), scales=lin_scales[a, c][:], in_=lin[a, c][:])
-            q_sq(a, c, 1)
+        for piece in (x00, x10, x01):
+            a, c = piece[:2]
+            cast_sq(piece, 0)
+            cast_sq(piece, 1)
+            cast_lin(piece, 0)
+            if piece == x01:
+                cast_lin(piece, 1, 0, P // 2)
+                cast_lin_scalar(piece, 1, P // 2, P)
+                q_sq(a, c, 0, 2)
+                q_lin(a, c, 0, 2)
+            else:
+                cast_lin(piece, 1)
+                q_sq(a, c, 0, 2)
+                q_lin(a, c, 0, 4)
+            q_sq(a, c, 2, 4)
             if c == 0:
                 for r in range(PACK):
                     pass_sq(a, 0, r)
@@ -220,26 +244,29 @@ def tile_mix_feat_tm_quadpl_mul_kernel(
             for r in range(PACK):
                 pass_lin(a, 0, r)
 
-        cast_sq(1, 1, 0)
-        cast_sq(1, 1, 1)
-        cast_lin_scalar(1, 1, 1)
-        cast_lin(1, 1, 0)
+        def both(a, c, r):
+            pass_lin(a, c, r)
+            pass_sq(a, c, r, stop=True)
+
+        cast_sq(x11, 0)
+        cast_sq(x11, 1)
+        cast_lin_scalar(x11, 1)
+        cast_lin(x11, 0)
+        q_lin(0, 1, 2, 4)
         for r in range(PACK):
             both(0, 1, r)
-        q_lin(1, 1, 0)
-        q_sq(1, 1, 0)
+        q_lin(1, 1, 0, 2)
+        q_sq(1, 1, 0, 2)
         both(1, 1, 0)
         both(1, 1, 1)
-        H = M // 2
-        Q3 = 3 * M // 4 + 32
         gate_result(0, 0)
         gate_result(0, 1)
-        q_sq(1, 1, 1)
+        q_sq(1, 1, 2, 4)
         gate_result(0, 2, 0, H)
         store_result(0, 0, 2 * M + H)
         gate_result(0, 3, 0, H)
         round_scalar(0, 0, H)
-        q_lin(1, 1, 1)
+        q_lin(1, 1, 2, 4)
         both(1, 1, 2)
         both(1, 1, 3)
         gate_result(0, 2, H, M)
@@ -263,8 +290,4 @@ def tile_mix_feat_tm_quadpl_mul_kernel(
         quantize_result(1, 0, H)
         quantize_result(1, H, M)
         store_codes(1, 0, M)
-        for q in range(4):
-            nc.scalar.dma_start(
-                out=out_2[:, 4 * q:4 * q + 4, :].bitcast(I32),
-                in_=res_plane[32 * q + RES_ROW:32 * q + RES_ROW + 8, :].bitcast(I32),
-            )
+        store_scales()

@@ -261,18 +261,20 @@ def tile_mix_feat_tm_quadpl_mul_kernel(
         both(1, 1, 1)
         gate_result(0, 0)
         gate_result(0, 1)
+        store_result(0, 0, 2 * M)
         q_sq(1, 1, 2, 4)
+        for r in (2, 3):
+            pass_sq(1, 1, r)
         gate_result(0, 2, 0, H)
-        store_result(0, 0, 2 * M + H)
         gate_result(0, 3, 0, H)
         round_scalar(0, 0, H)
-        q_lin(1, 1, 2, 4)
-        both(1, 1, 2)
-        both(1, 1, 3)
         gate_result(0, 2, H, M)
         gate_result(0, 3, H, M)
-        store_result(0, 2 * M + H, 4 * M)
+        store_result(0, 2 * M, 4 * M)
         round_scalar(0, H, M)
+        q_lin(1, 1, 2, 4)
+        for r in (2, 3):
+            pass_lin(1, 1, r, stop=True)
         gate_result(1, 0)
         store_result(1, 0, M)
         gate_result(1, 1)

@@ -80,9 +80,9 @@ def tile_mix_feat_tm_quadpl_mul_kernel(
             return view[:, lo:hi, :]
 
         def load_w4_plane():
-            by_row = w4_scales.rearrange("c (q r) n -> r q c n", r=4)
-            for r in range(4):
-                nc.sync.dma_start(out=w4_plane[r:P:32, :, :].bitcast(I32), in_=by_row[r].bitcast(I32))
+            by_quadrant = w4_scales.rearrange("c (q r) n -> q r c n", r=4)
+            for q in (0, 2, 1, 3):
+                nc.sync.dma_start(out=w4_plane[32 * q:32 * q + 4, :, :].bitcast(I32), in_=by_quadrant[q].bitcast(I32))
 
         def load_w8_plane():
             for q in (0, 2, 1, 3):

@@ -38,10 +38,10 @@ def tile_mix_feat_tm_quadpl_mul_kernel(
         pieces = [(0, 0, 0, P), (1, 0, 0, P), (0, 1, 0, P), (1, 1, 0, P)]
 
         def tiles(name, keys, shape, dtype):
-            return {k: sb.tile(shape, dtype, name="%s_%s" % (name, i), align_bytes=64) for i, k in enumerate(keys)}
+            return {k: sb.tile(shape, dtype, name="%s_%s" % (name, i), align_bytes=256) for i, k in enumerate(keys)}
 
         raw = {
-            k: sb.tile([P, PACK, PACK * (k[3] - k[2])], F32, name="raw_%d" % i, align_bytes=64)
+            k: sb.tile([P, PACK, PACK * (k[3] - k[2])], F32, name="raw_%d" % i, align_bytes=256)
             for i, k in enumerate(pieces)
         }
         lin = tiles("lin", chunks, [P, PACK * SPAN], BF16)
@@ -51,16 +51,16 @@ def tile_mix_feat_tm_quadpl_mul_kernel(
         sq_codes = tiles("sq_codes", chunks, [P, SPAN], U32)
         sq_scales = tiles("sq_scales", chunks, [P, SPAN], U8)
         w8 = tiles("w8", range(PASSES), [P, M], U32)
-        w4 = sb.tile([P, PASSES * 2 * M], U8, align_bytes=64)
-        w4_plane_tile = sb.tile([P, PASSES * M + 2 * SHIFT], U8, align_bytes=64)
-        w8_plane_tile = sb.tile([P, M + 2 * SHIFT], U8, align_bytes=64)
+        w4 = sb.tile([P, PASSES * 2 * M], U8, align_bytes=256)
+        w4_plane_tile = sb.tile([P, PASSES * M + 2 * SHIFT], U8, align_bytes=256)
+        w8_plane_tile = sb.tile([P, M + 2 * SHIFT], U8, align_bytes=256)
         w4_plane = w4_plane_tile[:, SHIFT:SHIFT + PASSES * M].rearrange("p (c n) -> p c n", c=PASSES)
         w8_plane = w8_plane_tile[:, SHIFT:SHIFT + M]
         gate = tiles("gate", range(GROUPS), [P, PACK, M], F32)
         res = tiles("res", range(GROUPS), [P, PACK, M], F32)
         res_bf = tiles("res_bf", range(GROUPS), [P, M * PACK], BF16)
         res_codes = tiles("res_codes", range(GROUPS), [P, M], U32)
-        res_plane = sb.tile([P, M], U8, align_bytes=64)
+        res_plane = sb.tile([P, M], U8, align_bytes=256)
         acc = {(a, r): ps.tile([P, M], F32, name="acc_%d_%d" % (a, r)) for a in range(GROUPS) for r in range(PACK)}
 
         def load_x(piece):

@@ -22,7 +22,6 @@ PASSES = K // SPAN
 GROUPS = T // SPAN
 W8_ROW = 4
 RES_ROW = 8
-SHIFT = 128
 
 
 def tile_mix_feat_tm_quadpl_mul_kernel(
@@ -52,10 +51,10 @@ def tile_mix_feat_tm_quadpl_mul_kernel(
         sq_scales = tiles("sq_scales", chunks, [P, SPAN], U8)
         w8 = tiles("w8", range(PASSES), [P, M], U32)
         w4 = sb.tile([P, PASSES * 2 * M], U8, align_bytes=256)
-        w4_plane_tile = sb.tile([P, PASSES * M + 2 * SHIFT], U8, align_bytes=256)
-        w8_plane_tile = sb.tile([P, M + 2 * SHIFT], U8, align_bytes=256)
-        w4_plane = w4_plane_tile[:, SHIFT:SHIFT + PASSES * M].rearrange("p (c n) -> p c n", c=PASSES)
-        w8_plane = w8_plane_tile[:, SHIFT:SHIFT + M]
+        w4_plane_tile = sb.tile([P, PASSES * M], U8, align_bytes=256)
+        w8_plane_tile = sb.tile([P, M], U8, align_bytes=256)
+        w4_plane = w4_plane_tile[:].rearrange("p (c n) -> p c n", c=PASSES)
+        w8_plane = w8_plane_tile[:]
         gate = tiles("gate", range(GROUPS), [P, PACK, M], F32)
         res = tiles("res", range(GROUPS), [P, PACK, M], F32)
         res_bf = tiles("res_bf", range(GROUPS), [P, M * PACK], BF16)

from contextlib import ExitStack

import concourse.mybir as mybir

K, M, T = 1024, 512, 1024
FLOPS = 2 * 2 * K * M * T

F32 = mybir.dt.float32
BF16 = mybir.dt.bfloat16
I32 = mybir.dt.int32
U32 = mybir.dt.uint32
U8 = mybir.dt.uint8
FP8X4 = mybir.dt.float8_e4m3fn_x4
FP4X4 = mybir.dt.float4_e2m1fn_x4
ACT = mybir.ActivationFunctionType
ALU = mybir.AluOpType

P = 128
PACK = 4
SPAN = P * PACK
PASSES = K // SPAN
GROUPS = T // SPAN
W8_ROW = 4
RES_ROW = 8


def tile_mix_feat_tm_quadpl_mul_kernel(
    tc, x, w4_words, w4_scales, w8_words, w8_scales, g, out_0, out_1, out_2
):
    nc = tc.nc
    with ExitStack() as ctx:
        sb = ctx.enter_context(tc.tile_pool(name="sb", bufs=1))
        ps = ctx.enter_context(tc.psum_pool(name="ps", bufs=1))
        ctx.enter_context(tc.manual_schedule())

        chunks = [(a, c) for c in range(PASSES) for a in range(GROUPS)]
        pieces = [(0, 0, 0, P), (1, 0, 0, P), (0, 1, 0, P), (1, 1, 0, P)]

        def tiles(name, keys, shape, dtype):
            return {k: sb.tile(shape, dtype, name="%s_%s" % (name, i), align_bytes=256) for i, k in enumerate(keys)}

        raw = {
            k: sb.tile([P, PACK, PACK * (k[3] - k[2])], F32, name="raw_%d" % i, align_bytes=256)
            for i, k in enumerate(pieces)
        }
        lin = tiles("lin", chunks, [P, PACK * SPAN], BF16)
        sq = tiles("sq", chunks, [P, PACK * SPAN], BF16)
        lin_codes = tiles("lin_codes", chunks, [P, SPAN], U32)
        lin_scales = tiles("lin_scales", chunks, [P, SPAN], U8)
        sq_codes = tiles("sq_codes", chunks, [P, SPAN], U32)
        sq_scales = tiles("sq_scales", chunks, [P, SPAN], U8)
        w8 = tiles("w8", range(PASSES), [P, M], U32)
        w4 = sb.tile([P, PASSES * 2 * M], U8, align_bytes=256)
        w4_plane_tile = sb.tile([P, PASSES * M], U8, align_bytes=256)
        w8_plane_tile = sb.tile([P, M], U8, align_bytes=256)
        w4_plane = w4_plane_tile[:].rearrange("p (c n) -> p c n", c=PASSES)
        w8_plane = w8_plane_tile[:]
        gate = tiles("gate", range(GROUPS), [P, PACK, M], F32)
        res = tiles("res", range(GROUPS), [P, PACK, M], F32)
        res_bf = tiles("res_bf", range(GROUPS), [P, M * PACK], BF16)
        res_codes = tiles("res_codes", range(GROUPS), [P, M], U32)
        res_plane = sb.tile([P, M], U8, align_bytes=256)
        acc = {(a, r): ps.tile([P, M], F32, name="acc_%d_%d" % (a, r)) for a in range(GROUPS) for r in range(PACK)}

        def load_x(piece):
            a, c, lo, hi = piece
            rows = x[c * SPAN:(c + 1) * SPAN, a * SPAN + PACK * lo:a * SPAN + PACK * hi]
            nc.sync.dma_start(out=raw[piece][:], in_=rows.rearrange("(p j) t -> p j t", j=PACK))

        def load_w8(c):
            nc.sync.dma_start(out=w8[c][:].bitcast(I32), in_=w8_words[c].rearrange("p n i -> p (n i)").bitcast(I32))

        def load_w4(lo, hi):
            out = w4[:].bitcast(I32).rearrange("p (c n) -> p c n", c=PASSES)
            nc.sync.dma_start(out=out[:, lo:hi, :], in_=w4_words.bitcast(I32).rearrange("c p n -> p c n")[:, lo:hi, :])

        def token_rows(dram, a, lo, hi):
            view = dram[a * SPAN:(a + 1) * SPAN, :].rearrange("(p r) n -> p r n", r=PACK)
            return view[:, lo:hi, :]

        def load_w4_plane():
            by_quadrant = w4_scales.rearrange("c (q r) n -> q r c n", r=4)
            for q in (0, 2, 1, 3):
                nc.sync.dma_start(out=w4_plane[32 * q:32 * q + 4, :, :].bitcast(I32), in_=by_quadrant[q].bitcast(I32))

        def load_w8_plane():
            for q in (0, 2, 1, 3):
                nc.sync.dma_start(
                    out=w8_plane[32 * q + W8_ROW:32 * q + W8_ROW + 8, :].bitcast(I32),
                    in_=w8_scales[:, 4 * q:4 * q + 4, :].bitcast(I32),
                )

        def dealt(piece, half, lo=None, hi=None):
            a, c, first, last = piece
            lo, hi = (first, last) if lo is None else (lo, hi)
            pair = slice(2 * half, 2 * half + 2)
            src = raw[piece][:].rearrange("p j (m r) -> p m j r", r=PACK)[:, lo - first:hi - first, :, pair]
            out = sq[a, c][:].rearrange("p (r m j) -> p m j r", r=PACK, j=PACK)[:, lo:hi, :, pair]
            return out, src

        def dealt_pairs(piece, half, lo=None, hi=None):
            a, c, first, last = piece
            lo, hi = (first, last) if lo is None else (lo, hi)
            pair = slice(2 * half, 2 * half + 2)
            src = raw[piece][:].rearrange("p (h l) (m r) -> p m h r l", l=2, r=PACK)[:, lo - first:hi - first, :, pair, :]
            out = lin[a, c][:].rearrange("p (r m h l) -> p m h r l", r=PACK, h=2, l=2)[:, lo:hi, :, pair, :]
            return out, src

        def cast_lin(piece, half, lo=None, hi=None):
            out, src = dealt_pairs(piece, half, lo, hi)
            nc.vector.tensor_copy(out=out, in_=src)

        def cast_lin_scalar(piece, half, lo=None, hi=None):
            out, src = dealt_pairs(piece, half, lo, hi)
            nc.scalar.copy(out=out, in_=src)

        def cast_sq(piece, half, lo=None, hi=None):
            out, src = dealt(piece, half, lo, hi)
            nc.scalar.activation(out=out, in_=src, func=ACT.Square)

        def quantize(src, codes, scales, a, c, lo, hi):
            cols = slice(lo * P, hi * P)
            nc.vector.quantize_mx(
                out=codes[a, c][:, cols].bitcast(FP8X4),
                scales=scales[a, c][:, cols],
                in_=src[a, c][:, PACK * cols.start:PACK * cols.stop],
            )

        def q_lin(a, c, lo, hi):
            quantize(lin, lin_codes, lin_scales, a, c, lo, hi)

        def q_sq(a, c, lo, hi):
            quantize(sq, sq_codes, sq_scales, a, c, lo, hi)

        def pass_lin(a, c, r, stop=False):
            cols = slice(r * P, (r + 1) * P)
            nc.tensor.matmul_mx(
                out=acc[a, r][:],
                lhsT=lin_codes[a, c][:, cols].bitcast(FP8X4),
                lhsT_scale=lin_scales[a, c][:, cols],
                rhs=w8[c][:].bitcast(FP8X4),
                rhs_scale=w8_plane[W8_ROW + 4 * c:P, :],
                start=False,
                stop=stop,
            )

        def pass_sq(a, c, r, stop=False):
            cols = slice(r * P, (r + 1) * P)
            nc.tensor.matmul_mx(
                out=acc[a, r][:],
                lhsT=sq_codes[a, c][:, cols].bitcast(FP8X4),
                lhsT_scale=sq_scales[a, c][:, cols],
                rhs=w4[:, 2 * M * c:2 * M * (c + 1)].bitcast(FP4X4),
                rhs_scale=w4_plane[:, c, :],
                start=(c == 0),
                stop=stop,
            )

        def gate_result(a, r, lo=0, hi=M):
            nc.vector.tensor_tensor(
                out=res[a][:, r, lo:hi], in0=acc[a, r][:, lo:hi], in1=gate[a][:, r, lo:hi], op=ALU.mult
            )

        def store_result(a, lo, hi):
            rows = out_0[a * SPAN:(a + 1) * SPAN, :].rearrange("(p r) n -> p (r n)", r=PACK)
            nc.sync.dma_start(out=rows[:, lo:hi], in_=res[a][:].rearrange("p r n -> p (r n)")[:, lo:hi])

        def interleaved(a, lo, hi):
            src = res[a][:, :, lo:hi].rearrange("p (h l) (u i) -> p u h i l", l=2, i=4)
            out = res_bf[a][:, PACK * lo:PACK * hi].rearrange("p (u i h l) -> p u h i l", i=4, h=2, l=2)
            return out, src

        def round_scalar(a, lo, hi):
            out, src = interleaved(a, lo, hi)
            nc.scalar.copy(out=out, in_=src)

        def round_vector(a, lo, hi):
            out, src = interleaved(a, lo, hi)
            nc.vector.tensor_copy(out=out, in_=src)

        def quantize_result(a, lo, hi):
            nc.vector.quantize_mx(
                out=res_codes[a][:, lo:hi].bitcast(FP8X4),
                scales=res_plane[RES_ROW + 4 * a:P, lo:hi],
                in_=res_bf[a][:, PACK * lo:PACK * hi],
            )

        def store_codes(a, lo, hi):
            words = out_1[a].rearrange("p n i -> p (n i)").bitcast(I32)
            nc.sync.dma_start(out=words[:, lo:hi], in_=res_codes[a][:, lo:hi].bitcast(I32))

        def load_gate(a, lo, hi):
            nc.sync.dma_start(out=gate[a][:, lo:hi, :], in_=token_rows(g, a, lo, hi))

        def store_scales():
            for q in range(4):
                nc.scalar.dma_start(
                    out=out_2[:, 4 * q:4 * q + 4, :].bitcast(I32),
                    in_=res_plane[32 * q + RES_ROW:32 * q + RES_ROW + 8, :].bitcast(I32),
                )

        H = M // 2
        Q3 = 3 * M // 4 + 32
        x00, x10, x01, x11 = pieces

        nc.vector.memset(w4_plane.bitcast(I32), 0)
        nc.vector.memset(w8_plane.bitcast(I32), 0)
        load_x(x00)
        load_w4(0, 1)
        load_w4_plane()
        load_x(x10)
        load_x(x01)
        load_w8(0)
        load_w8_plane()
        load_x(x11)
        load_w8(1)
        load_w4(1, 2)
        load_gate(0, 0, 1)
        load_gate(0, 1, 2)
        load_gate(0, 2, 4)
        load_gate(1, 0, 2)
        load_gate(1, 2, 4)

        for piece in (x00, x10, x01):
            a, c = piece[:2]
            cast_sq(piece, 0)
            cast_sq(piece, 1)
            cast_lin(piece, 0)
            if piece == x01:
                cast_lin(piece, 1, 0, P // 2)
                cast_lin_scalar(piece, 1, P // 2, P)
                q_sq(a, c, 0, 2)
                q_lin(a, c, 0, 2)
            else:
                cast_lin(piece, 1)
                q_sq(a, c, 0, 2)
                q_lin(a, c, 0, 4)
            q_sq(a, c, 2, 4)
            if c == 0:
                for r in range(PACK):
                    pass_sq(a, 0, r)
        for a in range(GROUPS):
            for r in range(PACK):
                pass_lin(a, 0, r)

        def both(a, c, r):
            pass_lin(a, c, r)
            pass_sq(a, c, r, stop=True)

        cast_sq(x11, 0)
        cast_sq(x11, 1)
        cast_lin_scalar(x11, 1)
        cast_lin(x11, 0)
        q_lin(0, 1, 2, 4)
        for r in range(PACK):
            both(0, 1, r)
        q_lin(1, 1, 0, 2)
        q_sq(1, 1, 0, 2)
        both(1, 1, 0)
        both(1, 1, 1)
        gate_result(0, 0)
        gate_result(0, 1)
        store_result(0, 0, 2 * M)
        q_sq(1, 1, 2, 4)
        for r in (2, 3):
            pass_sq(1, 1, r)
        gate_result(0, 2, 0, H)
        gate_result(0, 3, 0, H)
        round_scalar(0, 0, H)
        gate_result(0, 2, H, M)
        gate_result(0, 3, H, M)
        store_result(0, 2 * M, 4 * M)
        round_scalar(0, H, M)
        q_lin(1, 1, 2, 4)
        for r in (2, 3):
            pass_lin(1, 1, r, stop=True)
        gate_result(1, 0)
        store_result(1, 0, M)
        gate_result(1, 1)
        gate_result(1, 2, 0, H)
        store_result(1, M, 2 * M + H)
        gate_result(1, 3, 0, H)
        round_scalar(1, 0, H)
        gate_result(1, 2, H, M)
        gate_result(1, 3, H, M)
        store_result(1, 2 * M + H, 4 * M)
        round_scalar(1, Q3, M)
        quantize_result(0, 0, M)
        store_codes(0, 0, M)
        round_vector(1, H, Q3)
        quantize_result(1, 0, H)
        quantize_result(1, H, M)
        store_codes(1, 0, M)
        store_scales()
